import numpy as np, ml_dtypes
CORES = [17,81,89,18,82,90]
N = 6
import mx_ref
NC = 512
A = np.float32(0.03)
BF = ml_dtypes.bfloat16
def setup_inputs(rng):
    def f(*shape):
        return mx_ref.flush((rng.standard_normal(shape, dtype=np.float32) * np.exp2(rng.integers(-2, 3, shape[:-1] + (1,)))).astype(BF))
    return {"x": f(N, 128, 512), "w": f(N, 128, 4 * NC)}
def setup_inputs_blocks(rng):
    d = setup_inputs(rng)
    for k in ("x", "w"): d[k] = mx_ref.spread(d[k], rng, 2)
    return d
def setup_inputs_sharp(rng):
    d = setup_inputs(rng); d["w"] = (d["w"].astype(np.float32) * 32).astype(BF)
    return d
def setup_inputs_apart(rng):
    d = setup_inputs(rng); d["w"] = mx_ref.flush((d["w"].astype(np.float32) * np.exp2(rng.permutation(np.linspace(-3, 3, N))).astype(np.float32).reshape(N, 1, 1)).astype(BF))
    return d
def reference(x, w):
    W = [mx_ref.quantize(w[r]) for r in range(N)]
    y = np.zeros((N, 128, N * NC), np.float32)
    for j in range(N):
        X = mx_ref.quantize(x[j])
        L = [(mx_ref.matmul(X, W[r]) * A).astype(np.float64) for r in range(N)]
        m = np.max([l.max(axis=1, keepdims=True) for l in L], axis=0); s = sum(np.exp(l - m).sum(axis=1, keepdims=True) for l in L)
        for r in range(N):
            y[r][:, NC * j:NC * j + NC] = (np.exp(L[r] - m) / s).astype(np.float32)
    return {"y": y}

@@ -1,0 +1,267 @@
+import numpy as np
+import math
+from concourse.bass import DstId, RemoteDMATransfer
+from concourse.mybir import dt, AluOpType, AxisListType, ActivationFunctionType
+
+N = 6
+NC = 512
+XW = 128
+A = 0.03
+NB = N // 2
+NF = 2 * NB
+PAD = (-NF) % 4
+TABW = PAD + N * NF + 2
+
+SCRATCH = {
+    "xt": ("sbuf", [128, 4 * XW], "bfloat16"),
+    "wt": ("sbuf", [128, 4 * NC], "bfloat16"),
+    "xc": ("sbuf", [128, N * XW], "float8_e4m3fn_x4"),
+    "xs": ("sbuf", [128, N * XW], "uint8"),
+    "wc": ("sbuf", [128, NC], "float8_e4m3fn_x4"),
+    "ws": ("sbuf", [128, NC], "uint8"),
+    "ps": ("psum", [128, N * NC], "float32"),
+    "e": ("sbuf", [128, N * NC], "float32"),
+    "raw": ("sbuf", [128, 8], "float32"),
+    "tab0": ("sbuf", [128, TABW], "float32"),
+    "tab1": ("sbuf", [128, TABW], "float32"),
+    "own0": ("sbuf", [128, 8], "float32"),
+    "own1": ("sbuf", [128, 8], "float32"),
+    "wk0": ("sbuf", [128, 64], "float32"),
+    "wk1": ("sbuf", [128, 64], "float32"),
+}
+SEMAPHORES = (["xl", "wl", "xq", "wq", "snt", "yst"]
+              + ["%s%d" % (n, j) for n in ("xa", "mm", "mx", "ng", "ex") for j in range(N)]
+              + ["%s%d" % (n, b) for n in ("pp", "st", "gm", "ee", "pm", "sm", "rc", "ff", "sa", "sb", "sc")
+                 for b in range(2)])
+
+
+def _pop(m):
+    return sum((m >> b) & 1 for b in range(m.bit_length()))
+
+
+def _plan(T, topo):
+    cores = list(T.cores)
+    chips = sorted(set(topo.chip(c) for c in cores))
+    port, door = {}, {}
+    for ch in chips:
+        mem = [c for c in cores if topo.chip(c) == ch]
+        ok = [m for m in mem if all(topo.may_write(m, d) for d in cores if d != m)]
+        port[ch] = ok[0]
+        door[ch] = [m for m in mem if m != ok[0]][0]
+
+    def hop(a, b):
+        ca, cb = topo.chip(a), topo.chip(b)
+        if ca == cb:
+            return 1.0
+        return 1.5 if (topo.mates(ca, cb) or topo.same_plane(ca, cb)) else 1.7
+
+    def masks(c):
+        ch = topo.chip(c)
+        mate = port[ch] if c != port[ch] else door[ch]
+        far = [d for d in cores if topo.chip(d) != ch][0]
+        full, lo = topo.mask(c, mate), topo.mask(c, far)
+        return full, lo, full & ~lo
+
+    calls, arr, cnt = [], {}, {}
+
+    def add(src, j, ready, on, off):
+        full, lo, hi = masks(src)
+        trs = []
+        if off:
+            trs.append((lo, off))
+        if on:
+            trs.append((hi if off else full, on))
+        for m, ds in trs:
+            for d in ds:
+                arr[(j, d)] = ready + hop(src, d)
+                cnt[(j, d)] = 2 * _pop(m)
+        calls.append({"src": src, "tile": j, "ready": ready, "trs": trs})
+
+    for j, s in enumerate(cores):
+        cs = topo.chip(s)
+        p = port[cs] if s != port[cs] else door[cs]
+        arr[(j, s)] = 0.0
+        far = [ch for ch in chips if ch != cs]
+        direct = [ch for ch in far if topo.may_write(s, door[ch])]
+        add(s, j, 0.0, [p], [door[ch] for ch in direct])
+        rest = [ch for ch in far if ch not in direct]
+        if rest:
+            add(p, j, arr[(j, p)] + 0.5, [], [door[ch] for ch in rest])
+        for ch in far:
+            add(door[ch], j, arr[(j, door[ch])], [port[ch]], [])
+    early = [j for j, s in enumerate(cores) if s == port[topo.chip(s)]]
+    late = [j for j in range(len(cores)) if j not in early]
+    return {"cores": cores, "chips": chips, "port": port, "door": door, "calls": calls, "arr": arr, "cnt": cnt,
+            "batches": [early, late], "masks": masks}
+
+
+def rank_program(g, core, T, topo):
+    rank = T.rank_of(core)
+    if rank is None:
+        return
+    P = _plan(T, topo)
+    cores, chips, arr, cnt = P["cores"], P["chips"], P["arr"], P["cnt"]
+    ch = topo.chip(core)
+    is_port = core == P["port"][ch]
+    partner = P["door"][ch] if is_port else P["port"][ch]
+    full, lo, hi = P["masks"](core)
+    S = T.sem
+    sent = [0]
+    Exp, Copy = ActivationFunctionType.Exp, ActivationFunctionType.Copy
+    MULT, MIN, MAX, ADD = AluOpType.mult, AluOpType.min, AluOpType.max, AluOpType.add
+    X = AxisListType.X
+
+    def did(c):
+        rid, pid, _ = topo.addr(c)
+        return DstId(rid=rid, pnc=pid)
+
+    def blk(j):
+        return slice(NC * j, NC * j + NC)
+
+    def xsl(j):
+        return slice(XW * j, XW * j + XW)
+
+    def own_col(b, jp, t):
+        if is_port:
+            c = PAD + 2 * jp + t
+            return T["tab%d" % b][:, c:c + 1]
+        c = 2 * jp + t
+        return T["own%d" % b][:, c:c + 1]
+
+    where = {}
+    for b, bl in enumerate(P["batches"]):
+        for jp, j in enumerate(bl):
+            where[j] = (b, jp)
+
+    g.sync.dma_start(T.xt[:], T.x[:]).then_inc(S.xl, 16)
+    g.sync.dma_start(T.wt[:], T.w[:]).then_inc(S.wl, 16)
+
+    g.vector.wait_ge(S.xl, 16)
+    g.vector.quantize_mx(T.xc[:, xsl(rank)], T.xs[:, xsl(rank)], T.xt[:]).then_inc(S.xq, 1)
+    g.vector.wait_ge(S.wl, 16)
+    g.vector.quantize_mx(T.wc[:], T.ws[:], T.wt[:]).then_inc(S.wq, 1)
+
+    order = sorted(range(N), key=lambda j: arr[(j, core)])
+    g.tensor.wait_ge(S.wq, 1)
+    for j in order:
+        if j == rank:
+            g.tensor.wait_ge(S.xq, 1)
+        else:
+            g.tensor.wait_ge(S["xa%d" % j], cnt[(j, core)])
+        g.tensor.matmul_mx(T.ps[:, blk(j)], T.xc[:, xsl(j)], T.xs[:, xsl(j)], T.wc[:], T.ws[:],
+                           True, True).then_inc(S["mm%d" % j], 1)
+    for j in order:
+        b, jp = where[j]
+        g.vector.wait_ge(S["mm%d" % j], 1)
+        g.vector.tensor_reduce(T.raw[:, j:j + 1], T.ps[:, blk(j)], X, MAX, negate=True).then_inc(S["mx%d" % j], 1)
+        g.vector.wait_ge(S["mx%d" % j], 1)
+        g.vector.tensor_scalar(own_col(b, jp, 0), T.raw[:, j:j + 1], A, None, MULT).then_inc(S["ng%d" % j], 1)
+    for j in order:
+        b, jp = where[j]
+        g.scalar.wait_ge(S["ng%d" % j], 1)
+        g.scalar.activation(T.e[:, blk(j)], T.ps[:, blk(j)], Exp, bias=own_col(b, jp, 0), scale=A,
+                            accum_out=own_col(b, jp, 1)).then_inc(S["ex%d" % j], 1)
+
+    items = []
+    for c in P["calls"]:
+        if c["src"] == core:
+            items.append((c["ready"], 0, "x", c))
+    for b, bl in enumerate(P["batches"]):
+        mine = max(arr[(j, core)] for j in bl) + 1.0
+        if is_port:
+            mine = max(mine, max(arr[(j, partner)] for j in bl) + 2.0)
+        items.append((mine, 1, "s", b))
+    items.sort(key=lambda it: (it[0], it[1]))
+
+    def slot(dst, src_chip):
+        dc = topo.chip(dst)
+        k = 0 if dc == src_chip else 1 + [c for c in chips if c != dc].index(src_chip)
+        return slice(PAD + 2 * NF * k, PAD + 2 * NF * (k + 1))
+
+    for _, _, kind, what in items:
+        if kind == "x":
+            j = what["tile"]
+            if j == rank:
+                g.wait_ge(S.xq, 1)
+            else:
+                g.wait_ge(S["xa%d" % j], cnt[(j, core)])
+            for view in (T.xc[:, xsl(j)].bitcast(dt.uint8), T.xs[:, xsl(j)]):
+                tl = [RemoteDMATransfer(dst_ids=[did(d) for d in ds], dma_engine_mask=m, remote_sem=S["xa%d" % j],
+                                        srcs=[view], dsts=[view for d in ds]) for m, ds in what["trs"]]
+                g.remote_dma_fused(tl, local_sem=S.snt)
+                sent[0] += sum(_pop(m) for m, ds in what["trs"])
+        else:
+            b = what
+            tab = T["tab%d" % b]
+            for j in P["batches"][b]:
+                g.wait_ge(S["ng%d" % j], 1)
+                g.wait_ge(S["ex%d" % j], 1)
+            if not is_port:
+                tl = [RemoteDMATransfer(dst_ids=[did(partner)], dma_engine_mask=full, remote_sem=S["pp%d" % b],
+                                        srcs=[T["own%d" % b][:, 0:NF]], dsts=[tab[:, PAD + NF:PAD + 2 * NF]])]
+                g.remote_dma_fused(tl, local_sem=S.snt)
+                sent[0] += _pop(full)
+            else:
+                g.wait_ge(S["pp%d" % b], _pop(P["masks"](partner)[0]))
+                far = [d for d in cores if topo.chip(d) != ch]
+                src = tab[:, slot(core, ch)]
+                tl = [RemoteDMATransfer(dst_ids=[did(d) for d in far], dma_engine_mask=lo, remote_sem=S["st%d" % b],
+                                        srcs=[src], dsts=[tab[:, slot(d, ch)] for d in far]),
+                      RemoteDMATransfer(dst_ids=[did(partner)], dma_engine_mask=hi, remote_sem=S["st%d" % b],
+                                        srcs=[src], dsts=[tab[:, slot(partner, ch)]])]
+                g.remote_dma_fused(tl, local_sem=S.snt)
+                sent[0] += _pop(lo) + _pop(hi)
+
+    stores = 0
+    for b, bl in enumerate(P["batches"]):
+        tab, wk = T["tab%d" % b], T["wk%d" % b]
+        got = 0
+        for c in chips:
+            if c != ch:
+                got += _pop(P["masks"](P["port"][c])[1])
+        if not is_port:
+            got += _pop(P["masks"](partner)[2])
+        for q in (g.vector, g.scalar):
+            q.wait_ge(S["st%d" % b], got)
+            if is_port:
+                q.wait_ge(S["pp%d" % b], _pop(P["masks"](partner)[0]))
+            for j in bl:
+                q.wait_ge(S["ex%d" % j], 1)
+        end = PAD + N * NF
+        me = 0 if is_port else 1
+        GM, EE, PM, SM, RC, FF = 0, 4, 24, 44, 48, 52
+        for jp in range(NB):
+            g.vector.tensor_reduce(wk[:, GM + jp:GM + jp + 1], tab[:, PAD + 2 * jp:end:NF], X, MIN
+                                   ).then_inc(S["gm%d" % b], 1)
+        g.scalar.wait_ge(S["gm%d" % b], NB)
+        for jp in range(NB):
+            g.scalar.activation(wk[:, EE + jp:EE + N * NB:NB], tab[:, PAD + 2 * jp:end:NF], Exp,
+                                bias=wk[:, GM + jp:GM + jp + 1], scale=-1.0).then_inc(S["ee%d" % b], 1)
+        g.vector.wait_ge(S["ee%d" % b], NB)
+        g.vector.tensor_tensor(wk[:, PM:PM + N * NB], tab[:, PAD + 1:end + 1:2], wk[:, EE:EE + N * NB], MULT
+                               ).then_inc(S["pm%d" % b], 1)
+        g.vector.wait_ge(S["pm%d" % b], 1)
+        for jp in range(NB):
+            g.vector.tensor_reduce(wk[:, SM + jp:SM + jp + 1], wk[:, PM + jp:PM + N * NB:NB], X, ADD
+                                   ).then_inc(S["sm%d" % b], 1)
+        g.vector.wait_ge(S["sm%d" % b], NB)
+        g.vector.reciprocal(wk[:, RC:RC + NB], wk[:, SM:SM + NB]).then_inc(S["rc%d" % b], 1)
+        g.vector.wait_ge(S["rc%d" % b], 1)
+        g.vector.tensor_tensor(wk[:, FF:FF + NB], wk[:, RC:RC + NB], wk[:, EE + NB * me:EE + NB * me + NB], MULT
+                               ).then_inc(S["ff%d" % b], 1)
+        g.vector.wait_ge(S["ff%d" % b], 1)
+        g.scalar.wait_ge(S["ff%d" % b], 1)
+        ja, jb, jc = bl
+        h = NC // 2
+        fa, fb, fc = (wk[:, FF + k:FF + k + 1] for k in range(NB))
+        g.vector.tensor_scalar(T.e[:, blk(ja)], T.e[:, blk(ja)], fa, None, MULT).then_inc(S["sa%d" % b], 1)
+        g.scalar.activation(T.e[:, blk(jb)], T.e[:, blk(jb)], Copy, scale=fb).then_inc(S["sb%d" % b], 1)
+        c0 = NC * jc
+        g.vector.tensor_scalar(T.e[:, c0:c0 + h], T.e[:, c0:c0 + h], fc, None, MULT).then_inc(S["sc%d" % b], 1)
+        g.scalar.activation(T.e[:, c0 + h:c0 + NC], T.e[:, c0 + h:c0 + NC], Copy, scale=fc).then_inc(S["sc%d" % b], 1)
+        for name, j, n in (("sa", ja, 1), ("sb", jb, 1), ("sc", jc, 2)):
+            g.sync.wait_ge(S["%s%d" % (name, b)], n)
+            g.sync.dma_start(T.y[:, blk(j)], T.e[:, blk(j)]).then_inc(S.yst, 16)
+            stores += 1
+    g.sync.wait_ge(S.yst, 16 * stores)
+    g.wait_ge(S.snt, sent[0])

@@ -11,6 +11,7 @@ NB = N // 2
 NF = 2 * NB
 PAD = (-NF) % 4
 TABW = PAD + N * NF + 2
+CAP = 75.0
 
 SCRATCH = {
     "xt": ("sbuf", [128, 4 * XW], "bfloat16"),
@@ -26,12 +27,12 @@ SCRATCH = {
     "tab1": ("sbuf", [128, TABW], "float32"),
     "own0": ("sbuf", [128, 8], "float32"),
     "own1": ("sbuf", [128, 8], "float32"),
-    "wk0": ("sbuf", [128, 64], "float32"),
-    "wk1": ("sbuf", [128, 64], "float32"),
+    "wk0": ("sbuf", [128, 80], "float32"),
+    "wk1": ("sbuf", [128, 80], "float32"),
 }
 SEMAPHORES = (["xl", "wl", "xq", "wq", "snt", "yst"]
               + ["%s%d" % (n, j) for n in ("xa", "mm", "mx", "ng", "ex") for j in range(N)]
-              + ["%s%d" % (n, b) for n in ("pp", "st", "gm", "ee", "pm", "sm", "rc", "ff", "sa", "sb", "sc")
+              + ["%s%d" % (n, b) for n in ("pp", "st", "gm", "ee", "pm", "sm", "ff", "sa", "sb", "sc")
                  for b in range(2)])
 
 
@@ -108,7 +109,7 @@ def rank_program(g, core, T, topo):
     S = T.sem
     sent = [0]
     Exp, Copy = ActivationFunctionType.Exp, ActivationFunctionType.Copy
-    MULT, MIN, MAX, ADD = AluOpType.mult, AluOpType.min, AluOpType.max, AluOpType.add
+    MULT, MAX, ADD, SUB = AluOpType.mult, AluOpType.max, AluOpType.add, AluOpType.subtract
     X = AxisListType.X
 
     def did(c):
@@ -228,40 +229,52 @@ def rank_program(g, core, T, topo):
             for j in bl:
                 q.wait_ge(S["ex%d" % j], 1)
         end = PAD + N * NF
-        me = 0 if is_port else 1
-        GM, EE, PM, SM, RC, FF = 0, 4, 24, 44, 48, 52
+        NV = N * NB
+        DD, EE, PM, SM, FF, JK = 0, 20, 40, 60, 64, 68
         for jp in range(NB):
-            g.vector.tensor_reduce(wk[:, GM + jp:GM + jp + 1], tab[:, PAD + 2 * jp:end:NF], X, MIN
-                                   ).then_inc(S["gm%d" % b], 1)
+            g.vector.tensor_scalar(wk[:, DD + jp:DD + NV:NB], tab[:, PAD + 2 * jp:end:NF], own_col(b, jp, 0), -CAP,
+                                   SUB, MAX).then_inc(S["gm%d" % b], 1)
         g.scalar.wait_ge(S["gm%d" % b], NB)
-        for jp in range(NB):
-            g.scalar.activation(wk[:, EE + jp:EE + N * NB:NB], tab[:, PAD + 2 * jp:end:NF], Exp,
-                                bias=wk[:, GM + jp:GM + jp + 1], scale=-1.0).then_inc(S["ee%d" % b], 1)
-        g.vector.wait_ge(S["ee%d" % b], NB)
-        g.vector.tensor_tensor(wk[:, PM:PM + N * NB], tab[:, PAD + 1:end + 1:2], wk[:, EE:EE + N * NB], MULT
+        g.scalar.activation(wk[:, EE:EE + NV], wk[:, DD:DD + NV], Exp, scale=-1.0).then_inc(S["ee%d" % b], 1)
+        g.vector.wait_ge(S["ee%d" % b], 1)
+        g.vector.tensor_tensor(wk[:, PM:PM + NV], tab[:, PAD + 1:end + 1:2], wk[:, EE:EE + NV], MULT
                                ).then_inc(S["pm%d" % b], 1)
         g.vector.wait_ge(S["pm%d" % b], 1)
-        for jp in range(NB):
-            g.vector.tensor_reduce(wk[:, SM + jp:SM + jp + 1], wk[:, PM + jp:PM + N * NB:NB], X, ADD
+        g.scalar.wait_ge(S["pm%d" % b], 1)
+        for jp in range(NB - 1):
+            g.vector.tensor_reduce(wk[:, SM + jp:SM + jp + 1], wk[:, PM + jp:PM + NV:NB], X, ADD
                                    ).then_inc(S["sm%d" % b], 1)
+        jp = NB - 1
+        g.scalar.activation(wk[:, JK:JK + N], wk[:, PM + jp:PM + NV:NB], Copy,
+                            accum_out=wk[:, SM + jp:SM + jp + 1]).then_inc(S["sm%d" % b], 1)
         g.vector.wait_ge(S["sm%d" % b], NB)
-        g.vector.reciprocal(wk[:, RC:RC + NB], wk[:, SM:SM + NB]).then_inc(S["rc%d" % b], 1)
-        g.vector.wait_ge(S["rc%d" % b], 1)
-        g.vector.tensor_tensor(wk[:, FF:FF + NB], wk[:, RC:RC + NB], wk[:, EE + NB * me:EE + NB * me + NB], MULT
-                               ).then_inc(S["ff%d" % b], 1)
+        g.vector.reciprocal(wk[:, FF:FF + NB], wk[:, SM:SM + NB]).then_inc(S["ff%d" % b], 1)
         g.vector.wait_ge(S["ff%d" % b], 1)
         g.scalar.wait_ge(S["ff%d" % b], 1)
-        ja, jb, jc = bl
-        h = NC // 2
-        fa, fb, fc = (wk[:, FF + k:FF + k + 1] for k in range(NB))
-        g.vector.tensor_scalar(T.e[:, blk(ja)], T.e[:, blk(ja)], fa, None, MULT).then_inc(S["sa%d" % b], 1)
-        g.scalar.activation(T.e[:, blk(jb)], T.e[:, blk(jb)], Copy, scale=fb).then_inc(S["sb%d" % b], 1)
-        c0 = NC * jc
-        g.vector.tensor_scalar(T.e[:, c0:c0 + h], T.e[:, c0:c0 + h], fc, None, MULT).then_inc(S["sc%d" % b], 1)
-        g.scalar.activation(T.e[:, c0 + h:c0 + NC], T.e[:, c0 + h:c0 + NC], Copy, scale=fc).then_inc(S["sc%d" % b], 1)
-        for name, j, n in (("sa", ja, 1), ("sb", jb, 1), ("sc", jc, 2)):
-            g.sync.wait_ge(S["%s%d" % (name, b)], n)
-            g.sync.dma_start(T.y[:, blk(j)], T.e[:, blk(j)]).then_inc(S.yst, 16)
+        fcol = {}
+        for k, j in enumerate(bl):
+            fcol[j] = wk[:, FF + k:FF + k + 1]
+        j0 = min(bl)
+        if sorted(bl) == list(range(j0, j0 + NB)):
+            pieces = [(NC * j0, NC * (j0 + 1)), (NC * (j0 + 1), NC * (j0 + NB))]
+        else:
+            pieces = [(NC * j, NC * (j + 1)) for j in bl]
+        for name, (lo_c, hi_c) in zip(("sa", "sb", "sc"), pieces):
+            sem = S["%s%d" % (name, b)]
+            mid = (lo_c + hi_c) // 2
+            n = 0
+            for on_vector, u, v in ((True, lo_c, mid), (False, mid, hi_c)):
+                while u < v:
+                    j = u // NC
+                    t = min(v, NC * (j + 1))
+                    if on_vector:
+                        g.vector.tensor_scalar(T.e[:, u:t], T.e[:, u:t], fcol[j], None, MULT).then_inc(sem, 1)
+                    else:
+                        g.scalar.activation(T.e[:, u:t], T.e[:, u:t], Copy, scale=fcol[j]).then_inc(sem, 1)
+                    n += 1
+                    u = t
+            g.sync.wait_ge(sem, n)
+            g.sync.dma_start(T.y[:, lo_c:hi_c], T.e[:, lo_c:hi_c]).then_inc(S.yst, 16)
             stores += 1
     g.sync.wait_ge(S.yst, 16 * stores)
     g.wait_ge(S.snt, sent[0])

import numpy as np
import math
from concourse.bass import DstId, RemoteDMATransfer
from concourse.mybir import dt, AluOpType, AxisListType, ActivationFunctionType

N = 6
NC = 512
XW = 128
A = 0.03
NB = N // 2
NF = 2 * NB
PAD = (-NF) % 4
TABW = PAD + N * NF + 2
CAP = 75.0

SCRATCH = {
    "xt": ("sbuf", [128, 4 * XW], "bfloat16"),
    "wt": ("sbuf", [128, 4 * NC], "bfloat16"),
    "xc": ("sbuf", [128, N * XW], "float8_e4m3fn_x4"),
    "xs": ("sbuf", [128, N * XW], "uint8"),
    "wc": ("sbuf", [128, NC], "float8_e4m3fn_x4"),
    "ws": ("sbuf", [128, NC], "uint8"),
    "ps": ("psum", [128, N * NC], "float32"),
    "e": ("sbuf", [128, N * NC], "float32"),
    "raw": ("sbuf", [128, 8], "float32"),
    "tab0": ("sbuf", [128, TABW], "float32"),
    "tab1": ("sbuf", [128, TABW], "float32"),
    "own0": ("sbuf", [128, 8], "float32"),
    "own1": ("sbuf", [128, 8], "float32"),
    "wk0": ("sbuf", [128, 80], "float32"),
    "wk1": ("sbuf", [128, 80], "float32"),
}
SEMAPHORES = (["xl", "wl", "xq", "wq", "snt", "yst"]
              + ["%s%d" % (n, j) for n in ("xa", "mm", "mx", "ng", "ex") for j in range(N)]
              + ["%s%d" % (n, b) for n in ("pp", "st", "gm", "ee", "pm", "sm", "ff", "sa", "sb", "sc")
                 for b in range(2)])


def _pop(m):
    return sum((m >> b) & 1 for b in range(m.bit_length()))


def _plan(T, topo):
    cores = list(T.cores)
    chips = sorted(set(topo.chip(c) for c in cores))
    port, door = {}, {}
    for ch in chips:
        mem = [c for c in cores if topo.chip(c) == ch]
        ok = [m for m in mem if all(topo.may_write(m, d) for d in cores if d != m)]
        port[ch] = ok[0]
        door[ch] = [m for m in mem if m != ok[0]][0]

    def hop(a, b):
        ca, cb = topo.chip(a), topo.chip(b)
        if ca == cb:
            return 1.0
        return 1.5 if (topo.mates(ca, cb) or topo.same_plane(ca, cb)) else 1.7

    def masks(c):
        ch = topo.chip(c)
        mate = port[ch] if c != port[ch] else door[ch]
        far = [d for d in cores if topo.chip(d) != ch][0]
        full, lo = topo.mask(c, mate), topo.mask(c, far)
        return full, lo, full & ~lo

    calls, arr, cnt = [], {}, {}

    def add(src, j, ready, on, off):
        full, lo, hi = masks(src)
        trs = []
        if off:
            trs.append((lo, off))
        if on:
            trs.append((hi if off else full, on))
        for m, ds in trs:
            for d in ds:
                arr[(j, d)] = ready + hop(src, d)
                cnt[(j, d)] = 2 * _pop(m)
        calls.append({"src": src, "tile": j, "ready": ready, "trs": trs})

    for j, s in enumerate(cores):
        cs = topo.chip(s)
        p = port[cs] if s != port[cs] else door[cs]
        arr[(j, s)] = 0.0
        far = [ch for ch in chips if ch != cs]
        direct = [ch for ch in far if topo.may_write(s, door[ch])]
        add(s, j, 0.0, [p], [door[ch] for ch in direct])
        rest = [ch for ch in far if ch not in direct]
        if rest:
            add(p, j, arr[(j, p)] + 0.5, [], [door[ch] for ch in rest])
        for ch in far:
            add(door[ch], j, arr[(j, door[ch])], [port[ch]], [])
    early = [j for j, s in enumerate(cores) if s == port[topo.chip(s)]]
    late = [j for j in range(len(cores)) if j not in early]
    return {"cores": cores, "chips": chips, "port": port, "door": door, "calls": calls, "arr": arr, "cnt": cnt,
            "batches": [early, late], "masks": masks}


def rank_program(g, core, T, topo):
    rank = T.rank_of(core)
    if rank is None:
        return
    P = _plan(T, topo)
    cores, chips, arr, cnt = P["cores"], P["chips"], P["arr"], P["cnt"]
    ch = topo.chip(core)
    is_port = core == P["port"][ch]
    partner = P["door"][ch] if is_port else P["port"][ch]
    full, lo, hi = P["masks"](core)
    S = T.sem
    sent = [0]
    Exp, Copy = ActivationFunctionType.Exp, ActivationFunctionType.Copy
    MULT, MAX, ADD, SUB = AluOpType.mult, AluOpType.max, AluOpType.add, AluOpType.subtract
    X = AxisListType.X

    def did(c):
        rid, pid, _ = topo.addr(c)
        return DstId(rid=rid, pnc=pid)

    def blk(j):
        return slice(NC * j, NC * j + NC)

    def xsl(j):
        return slice(XW * j, XW * j + XW)

    def own_col(b, jp, t):
        if is_port:
            c = PAD + 2 * jp + t
            return T["tab%d" % b][:, c:c + 1]
        c = 2 * jp + t
        return T["own%d" % b][:, c:c + 1]

    where = {}
    for b, bl in enumerate(P["batches"]):
        for jp, j in enumerate(bl):
            where[j] = (b, jp)

    g.sync.dma_start(T.xt[:], T.x[:]).then_inc(S.xl, 16)
    g.sync.dma_start(T.wt[:], T.w[:]).then_inc(S.wl, 16)

    g.vector.wait_ge(S.xl, 16)
    g.vector.quantize_mx(T.xc[:, xsl(rank)], T.xs[:, xsl(rank)], T.xt[:]).then_inc(S.xq, 1)
    g.vector.wait_ge(S.wl, 16)
    g.vector.quantize_mx(T.wc[:], T.ws[:], T.wt[:]).then_inc(S.wq, 1)

    order = sorted(range(N), key=lambda j: arr[(j, core)])
    g.tensor.wait_ge(S.wq, 1)
    for j in order:
        if j == rank:
            g.tensor.wait_ge(S.xq, 1)
        else:
            g.tensor.wait_ge(S["xa%d" % j], cnt[(j, core)])
        g.tensor.matmul_mx(T.ps[:, blk(j)], T.xc[:, xsl(j)], T.xs[:, xsl(j)], T.wc[:], T.ws[:],
                           True, True).then_inc(S["mm%d" % j], 1)
    for j in order:
        b, jp = where[j]
        g.vector.wait_ge(S["mm%d" % j], 1)
        g.vector.tensor_reduce(T.raw[:, j:j + 1], T.ps[:, blk(j)], X, MAX, negate=True).then_inc(S["mx%d" % j], 1)
        g.vector.wait_ge(S["mx%d" % j], 1)
        g.vector.tensor_scalar(own_col(b, jp, 0), T.raw[:, j:j + 1], A, None, MULT).then_inc(S["ng%d" % j], 1)
    for j in order:
        b, jp = where[j]
        g.scalar.wait_ge(S["ng%d" % j], 1)
        g.scalar.activation(T.e[:, blk(j)], T.ps[:, blk(j)], Exp, bias=own_col(b, jp, 0), scale=A,
                            accum_out=own_col(b, jp, 1)).then_inc(S["ex%d" % j], 1)

    items = []
    for c in P["calls"]:
        if c["src"] == core:
            items.append((c["ready"], 0, "x", c))
    for b, bl in enumerate(P["batches"]):
        mine = max(arr[(j, core)] for j in bl) + 1.0
        if is_port:
            mine = max(mine, max(arr[(j, partner)] for j in bl) + 2.0)
        items.append((mine, 1, "s", b))
    items.sort(key=lambda it: (it[0], it[1]))

    def slot(dst, src_chip):
        dc = topo.chip(dst)
        k = 0 if dc == src_chip else 1 + [c for c in chips if c != dc].index(src_chip)
        return slice(PAD + 2 * NF * k, PAD + 2 * NF * (k + 1))

    for _, _, kind, what in items:
        if kind == "x":
            j = what["tile"]
            if j == rank:
                g.wait_ge(S.xq, 1)
            else:
                g.wait_ge(S["xa%d" % j], cnt[(j, core)])
            for view in (T.xc[:, xsl(j)].bitcast(dt.uint8), T.xs[:, xsl(j)]):
                tl = [RemoteDMATransfer(dst_ids=[did(d) for d in ds], dma_engine_mask=m, remote_sem=S["xa%d" % j],
                                        srcs=[view], dsts=[view for d in ds]) for m, ds in what["trs"]]
                g.remote_dma_fused(tl, local_sem=S.snt)
                sent[0] += sum(_pop(m) for m, ds in what["trs"])
        else:
            b = what
            tab = T["tab%d" % b]
            for j in P["batches"][b]:
                g.wait_ge(S["ng%d" % j], 1)
                g.wait_ge(S["ex%d" % j], 1)
            if not is_port:
                tl = [RemoteDMATransfer(dst_ids=[did(partner)], dma_engine_mask=full, remote_sem=S["pp%d" % b],
                                        srcs=[T["own%d" % b][:, 0:NF]], dsts=[tab[:, PAD + NF:PAD + 2 * NF]])]
                g.remote_dma_fused(tl, local_sem=S.snt)
                sent[0] += _pop(full)
            else:
                g.wait_ge(S["pp%d" % b], _pop(P["masks"](partner)[0]))
                far = [d for d in cores if topo.chip(d) != ch]
                src = tab[:, slot(core, ch)]
                tl = [RemoteDMATransfer(dst_ids=[did(d) for d in far], dma_engine_mask=lo, remote_sem=S["st%d" % b],
                                        srcs=[src], dsts=[tab[:, slot(d, ch)] for d in far]),
                      RemoteDMATransfer(dst_ids=[did(partner)], dma_engine_mask=hi, remote_sem=S["st%d" % b],
                                        srcs=[src], dsts=[tab[:, slot(partner, ch)]])]
                g.remote_dma_fused(tl, local_sem=S.snt)
                sent[0] += _pop(lo) + _pop(hi)

    stores = 0
    for b, bl in enumerate(P["batches"]):
        tab, wk = T["tab%d" % b], T["wk%d" % b]
        got = 0
        for c in chips:
            if c != ch:
                got += _pop(P["masks"](P["port"][c])[1])
        if not is_port:
            got += _pop(P["masks"](partner)[2])
        for q in (g.vector, g.scalar):
            q.wait_ge(S["st%d" % b], got)
            if is_port:
                q.wait_ge(S["pp%d" % b], _pop(P["masks"](partner)[0]))
            for j in bl:
                q.wait_ge(S["ex%d" % j], 1)
        end = PAD + N * NF
        NV = N * NB
        DD, EE, PM, SM, FF, JK = 0, 20, 40, 60, 64, 68
        for jp in range(NB):
            g.vector.tensor_scalar(wk[:, DD + jp:DD + NV:NB], tab[:, PAD + 2 * jp:end:NF], own_col(b, jp, 0), -CAP,
                                   SUB, MAX).then_inc(S["gm%d" % b], 1)
        g.scalar.wait_ge(S["gm%d" % b], NB)
        g.scalar.activation(wk[:, EE:EE + NV], wk[:, DD:DD + NV], Exp, scale=-1.0).then_inc(S["ee%d" % b], 1)
        g.vector.wait_ge(S["ee%d" % b], 1)
        g.vector.tensor_tensor(wk[:, PM:PM + NV], tab[:, PAD + 1:end + 1:2], wk[:, EE:EE + NV], MULT
                               ).then_inc(S["pm%d" % b], 1)
        g.vector.wait_ge(S["pm%d" % b], 1)
        g.scalar.wait_ge(S["pm%d" % b], 1)
        for jp in range(NB - 1):
            g.vector.tensor_reduce(wk[:, SM + jp:SM + jp + 1], wk[:, PM + jp:PM + NV:NB], X, ADD
                                   ).then_inc(S["sm%d" % b], 1)
        jp = NB - 1
        g.scalar.activation(wk[:, JK:JK + N], wk[:, PM + jp:PM + NV:NB], Copy,
                            accum_out=wk[:, SM + jp:SM + jp + 1]).then_inc(S["sm%d" % b], 1)
        g.vector.wait_ge(S["sm%d" % b], NB)
        g.vector.reciprocal(wk[:, FF:FF + NB], wk[:, SM:SM + NB]).then_inc(S["ff%d" % b], 1)
        g.vector.wait_ge(S["ff%d" % b], 1)
        g.scalar.wait_ge(S["ff%d" % b], 1)
        fcol = {}
        for k, j in enumerate(bl):
            fcol[j] = wk[:, FF + k:FF + k + 1]
        j0 = min(bl)
        if sorted(bl) == list(range(j0, j0 + NB)):
            pieces = [(NC * j0, NC * (j0 + 1)), (NC * (j0 + 1), NC * (j0 + NB))]
        else:
            pieces = [(NC * j, NC * (j + 1)) for j in bl]
        for name, (lo_c, hi_c) in zip(("sa", "sb", "sc"), pieces):
            sem = S["%s%d" % (name, b)]
            mid = (lo_c + hi_c) // 2
            n = 0
            for on_vector, u, v in ((True, lo_c, mid), (False, mid, hi_c)):
                while u < v:
                    j = u // NC
                    t = min(v, NC * (j + 1))
                    if on_vector:
                        g.vector.tensor_scalar(T.e[:, u:t], T.e[:, u:t], fcol[j], None, MULT).then_inc(sem, 1)
                    else:
                        g.scalar.activation(T.e[:, u:t], T.e[:, u:t], Copy, scale=fcol[j]).then_inc(sem, 1)
                    n += 1
                    u = t
            g.sync.wait_ge(sem, n)
            g.sync.dma_start(T.y[:, lo_c:hi_c], T.e[:, lo_c:hi_c]).then_inc(S.yst, 16)
            stores += 1
    g.sync.wait_ge(S.yst, 16 * stores)
    g.wait_ge(S.snt, sent[0])
